import numpy as np
import ml_dtypes


def mxq(x, axis, fmt="e4m3"):
    dtype, down = {"e4m3": (ml_dtypes.float8_e4m3fn, 7), "e5m2": (ml_dtypes.float8_e5m2, 14)}[fmt]
    v = np.moveaxis(np.asarray(x, np.float32).astype(ml_dtypes.bfloat16).astype(np.float64), axis, -1)
    blocks = v.reshape(v.shape[:-1] + (-1, 32))
    amax = np.abs(blocks).max(-1, keepdims=True)
    byte = np.maximum(np.where(amax > 0, np.frexp(amax)[1] - 1 + 127, 0) - down, 1)
    scale = np.exp2(byte - 127.0)
    codes = (blocks / scale).astype(np.float32).astype(dtype).astype(np.float64)
    return np.moveaxis((codes * scale).reshape(v.shape), -1, axis)


WIDE = False


def mx_kscale(k):
    if not WIDE:
        return np.ones(k)
    levels = np.array([10, -10, 5, -5, 0])
    if k % 512:
        return np.exp2(np.random.permutation(np.resize(levels, k // 32))).repeat(32)
    a = np.empty((k // 512, 16))
    for p in range(k // 512):
        a[p, :8] = np.random.permutation(np.resize(levels, 8))
        for g in range(8):
            far = levels[np.abs(levels - a[p, g]) >= 10]
            a[p, g + 8] = far[np.random.randint(len(far))]
    return np.exp2(a.ravel()).repeat(32)


BF16 = ml_dtypes.bfloat16


def bf(x):
    return np.asarray(x, np.float32).astype(BF16)


def f64(x):
    return np.asarray(x).astype(np.float64)


E2M1 = np.array([0.0, 0.5, 1.0, 1.5, 2.0, 3.0, 4.0, 6.0, -0.0, -0.5, -1.0, -1.5, -2.0, -3.0, -4.0, -6.0])


def pack_weight(w, fmt):
    k, n = w.shape
    w = f64(bf(w)).reshape(k // 32, 32, n)
    amax = np.abs(w).max(1)
    if fmt == "e4m3":
        byte = np.frexp(amax)[1] - 1 + 127 - 7
    else:
        mant, ex = np.frexp(amax / 6.0)
        byte = np.where(mant > 0.5, ex, ex - 1) + 127
    byte = np.clip(np.where(amax > 0, byte, 1), 1, 254)
    scaled = (w * np.exp2(127.0 - byte)[:, None, :]).reshape(k, n).astype(np.float32)
    by_word = np.ascontiguousarray(scaled.reshape(k // 512, 128, 4, n).transpose(0, 1, 3, 2))
    if fmt == "e4m3":
        words = by_word.astype(ml_dtypes.float8_e4m3fn).view(np.uint8)
    else:
        c = by_word.astype(ml_dtypes.float4_e2m1fn).view(np.uint8) & 0xF
        words = c[..., 0::2] | (c[..., 1::2] << 4)
    return np.ascontiguousarray(words), np.ascontiguousarray(byte.astype(np.uint8).reshape(k // 512, 16, n))


def unpack_weight(words, scales, fmt):
    g, p, n, _ = words.shape
    if fmt == "e4m3":
        vals = np.ascontiguousarray(words).view(ml_dtypes.float8_e4m3fn).astype(np.float64)
    else:
        nib = np.empty((g, p, n, 4), np.uint8)
        nib[..., 0::2] = words & 0xF
        nib[..., 1::2] = words >> 4
        vals = E2M1[nib]
    vals = vals * np.repeat(np.exp2(scales.astype(np.float64) - 127.0), 8, axis=1)[..., None]
    return vals.transpose(0, 1, 3, 2).reshape(g * 512, n)
def pack4(w):
    words, scales = pack_weight(w, "e2m1")
    return words.reshape(words.shape[0], 128, -1), scales


def unpack4(words, scales):
    return unpack_weight(words.reshape(words.shape[0], 128, -1, 2), scales, "e2m1")


T, KD, KO, V = 512, 1024, 2048, 2048


def setup_inputs():
    s, t = mx_kscale(KD), mx_kscale(KO)
    profile = 0.5 + np.random.random_sample(V)
    ad = np.random.standard_normal((KD, V)) ** 4 * profile / (3.0 * (KD + KO))
    ao = np.random.standard_normal((KO, V)) ** 4 * profile / (3.0 * (KD + KO))
    sens = ad.sum(0) + ao.sum(0)
    fd = 0.5 + np.random.exponential(1.0, (T, KD))
    fo = 0.5 + np.random.exponential(1.0, (T, KO))
    ao_words, ao_scales = pack4(ao / t[:, None])
    return {"x": bf(0.2 + np.random.exponential(1.0, (T, V))),
            "yd": bf(fd * np.random.standard_normal((T, KD)) ** 2 * s),
            "fd": bf(fd),
            "yo": bf(fo * np.random.standard_normal((T, KO)) ** 2 * t),
            "fo": bf(fo),
            "ad": bf(ad / s[:, None]),
            "ao_words": ao_words,
            "ao_scales": ao_scales,
            "sens": bf(sens)}


def reference(x, yd, fd, yo, fo, ad, ao_words, ao_scales, sens):
    rd = f64(yd) / f64(fd)
    ro = f64(yo) / f64(fo)
    direct = mxq(rd, 1, "e4m3") @ mxq(f64(ad), 0, "e4m3")
    oblique = mxq(ro, 1, "e4m3") @ unpack4(ao_words, ao_scales)
    back = direct + oblique
    return f64(x) * back / f64(sens)

@@ -1,0 +1,252 @@
+from contextlib import ExitStack
+
+import concourse.mybir as mybir
+from concourse.masks import make_identity
+
+F32 = mybir.dt.float32
+BF16 = mybir.dt.bfloat16
+U32 = mybir.dt.uint32
+I32 = mybir.dt.int32
+U8 = mybir.dt.uint8
+FP8X4 = mybir.dt.float8_e4m3fn_x4
+FP4X4 = mybir.dt.float4_e2m1fn_x4
+MULT = mybir.AluOpType.mult
+ACT = mybir.ActivationFunctionType
+
+P = 128
+FRAMES, KD, KO, VOXELS = 512, 1024, 2048, 2048
+FLOPS = 2 * FRAMES * (KD + KO) * VOXELS
+K_PASS = 512
+K_CHUNK = 1024
+M_TILES = FRAMES // P
+N = 512
+N_TILES = VOXELS // N
+CHUNKS = (KO + KD) // K_CHUNK
+OBLIQUE_CHUNKS = KO // K_CHUNK
+
+LOADS = "f00 y00 d00 f01 y01 y10 d01 x1 y11 f02 x0 y02 f12 f10 y12 d10 f11 d21 a1 s d11 a2 y21 y20 a3 f20 a0 f21 y32 f32 y22 f22 f31 x3 y30 x2 f30 y31 d31 d20 d30"
+SEQ = "N R0 T0.0 R1 T1.1 I0 V00 I1 T2.2 D0 T3.3 A00 I2 Q0 D1 V01 I3 R2 Q1 A01 R3 D2 D3 Q2 Q3 X00 T4.4 X01 T5.5 I4 X02 T6.6 X03 T7.7 I5 D4 X10 I6 Q4 D5 M004.0 T8.1 V10 I7 T9.2 Q5 I8 A10 M005.0 T10.3 D6 I9 D7 T11.4 Q6 M001.0 Q7 D8 M011.5 I10 M014.5 D9 M021.6 M031.7 Q8 M101.1 Q9 I11 D10 M111.2 M002.0 V11 M012.5 M022.6 S21 M032.7 M102.1 M112.2 Q10 M121.3 A11 M104.1 M003.0 D11 M013.5 M015.5 X11 M023.6 I12 M033.7 Q11 M103.1 A21 M105.1 M000.0 X12 I13 M010.5 M020.6 F00 M025.6 M030.7 F01 I14 M100.1 M110.2 D12 M113.2 M114.2 F10 I15 T12.4 M115.2 D13 M120.3 F11 M122.3 C12 T13.0 I16 Q12 M123.3 D14 M125.3 D15 M130.5 C13 T14.1 I17 D16 M131.5 T15.4 Q13 T16.2 X13 M132.5 C14 M133.5 D17 C15 M200.0 C16 M201.0 Q14 I18 Q15 T17.1 Q16 X20 M202.0 M203.0 X21 M204.0 C17 M210.4 I19 D18 M211.4 M212.4 Q17 X22 T18.2 M205.0 I20 D19 M213.4 M214.4 F20 T19.1 C18 M215.4 D20 C19 M220.0 I21 F21 M221.0 T20.2 Q18 M222.0 Q19 V20 C20 M223.0 I22 M225.0 M230.1 M231.1 M232.1 Q20 I23 M233.1 A20 M300.4 M301.4 D21 M024.6 S31 M124.3 D22 T21.2 M224.0 F02 M302.4 F12 T22.6 F22 M310.3 M311.3 D23 C21 M312.3 C22 M320.0 A31 S30 T23.2 M321.0 Q21 Q22 X23 M035.7 M135.5 X30 M235.1 M303.4 X31 M304.4 M313.3 X32 M314.3 C23 M322.0 M323.0 Q23 A30 M305.4 M315.3 F30 M324.0 M034.7 F31 M134.5 M234.1 F03 M325.0 M330.6 F13 M331.6 M332.6 F23 M333.6 M334.6 F32 M335.6 X33 F33"
+ACC_BANKS = 7
+T_BANKS = 4
+UNFUSED = (12, 13, 14, 15, 16, 17, 18, 19, 20, 21, 22, 23)
+FAST = True
+
+
+def tile_pet_mlem_update_s1_kernel(tc, x, yd, fd, yo, fo, ad, ao_words, ao_scales, sens, out):
+    nc = tc.nc
+    with ExitStack() as ctx:
+        keep = ctx.enter_context(tc.tile_pool(name="keep", bufs=1))
+        work = ctx.enter_context(tc.tile_pool(name="work", bufs=3))
+        psum = ctx.enter_context(tc.psum_pool(name="psum", bufs=1))
+
+        ident = keep.tile([P, P], F32, name="ident")
+        make_identity(nc, ident[:])
+        ident_bf = keep.tile([P, P], BF16, name="ident_bf")
+        make_identity(nc, ident_bf[:])
+        sens_rows = keep.tile([P, P], BF16, name="sens_rows")
+        nc.vector.memset(sens_rows[:], 0.0)
+        ao_sc = keep.tile([P, 4, VOXELS], U8, name="ao_sc", align_bytes=64)
+        nc.gpsimd.memset(ao_sc[:].rearrange("p g n -> p (g n)").bitcast(I32), 0)
+        warm = keep.tile([P, 1], F32, name="warm")
+        nc.vector.memset(warm[:], 1.0)
+        nc.scalar.activation(out=warm[:], in_=warm[:], func=ACT.Abs_reciprocal_sqrt)
+
+        y_t, f_t, ad_raw, ao_t, x_t = {}, {}, {}, {}, {}
+        nc.sync.dma_start(out=sens_rows[0:16, :], in_=sens.rearrange("(c p) -> c p", c=16))
+
+        def load_part(dst, oblique, direct, name, m, c):
+            src, col = (oblique, c) if c < OBLIQUE_CHUNKS else (direct, c - OBLIQUE_CHUNKS)
+            t = keep.tile([P, K_CHUNK], BF16, name=f"{name}{m}_{c}", align_bytes=64)
+            nc.sync.dma_start(
+                out=t[:], in_=src[m * P : (m + 1) * P, col * K_CHUNK : (col + 1) * K_CHUNK]
+            )
+            dst[m, c] = t
+
+        def load_ad(n, g):
+            a = keep.tile([P, 4, N], BF16, name=f"ad{n}_{g}", align_bytes=64)
+            nc.sync.dma_start(
+                out=a[:],
+                in_=ad[g * K_PASS : (g + 1) * K_PASS, n * N : (n + 1) * N].rearrange("(p j) w -> p j w", j=4),
+            )
+            ad_raw[n, g] = a
+
+        def load_ao(g):
+            w = keep.tile([P, 2 * VOXELS], U8, name=f"ao{g}", align_bytes=64)
+            nc.sync.dma_start(out=w[:].bitcast(I32), in_=ao_words[g].bitcast(I32))
+            ao_t[g] = w
+
+        def load_ao_scales():
+            for q in range(4):
+                nc.sync.dma_start(
+                    out=ao_sc[32 * q : 32 * q + 4, :, :].bitcast(I32),
+                    in_=ao_scales[:, 4 * q : 4 * q + 4, :].rearrange("g r n -> r g n").bitcast(I32),
+                )
+
+        def load_x(m):
+            t = keep.tile([P, VOXELS], BF16, name=f"x{m}", align_bytes=64)
+            nc.sync.dma_start(out=t[:], in_=x[m * P : (m + 1) * P, :])
+            x_t[m] = t
+
+        for tok in LOADS.split():
+            k, v = tok[0], [int(ch) for ch in tok[1:]]
+            if k == "f": load_part(f_t, fo, fd, "f", *v)
+            if k == "y": load_part(y_t, yo, yd, "y", *v)
+            if k == "d": load_ad(*v)
+            if k == "a": load_ao(*v)
+            if k == "s": load_ao_scales()
+            if k == "x": load_x(*v)
+
+        passes = [(m, g) for m in range(M_TILES) for g in range(6)]
+        bank_of, recip, grouped, prod, r_codes, r_scales = {}, {}, {}, {}, {}, {}
+        ad_grouped, ad_codes, ad_scales, acc, xs = {}, {}, {}, {}, {}
+        recip_sens = keep.tile([P, VOXELS], F32, name="recip_sens")
+        recip_col = keep.tile([P, 16], F32, name="recip_col")
+
+        def invert_sens():
+            sens_t = psum.tile([P, P], BF16, name="sens_t", tag="b7", bufs=1)
+            nc.tensor.transpose(sens_t[:], sens_rows[:], ident_bf[:])
+            nc.vector.reciprocal(out=recip_col[:], in_=sens_t[:, 0:16])
+
+        def spread_sens(n):
+            bank = psum.tile([P, 4, P], F32, name="s_bank", tag=f"b{7 - n}", bufs=1)
+            for i in range(4):
+                c = 4 * n + i
+                nc.tensor.transpose(bank[:, i, :], recip_col[:, c : c + 1].to_broadcast([P, P]), ident[:])
+            nc.scalar.copy(out=recip_sens[:, n * N : (n + 1) * N], in_=bank[:].rearrange("p i f -> p (i f)"))
+
+        def flip(i, bk):
+            m, g = passes[i]
+            if i in UNFUSED:
+                bank = psum.tile([P, 2, P], F32, name="p_bank", tag=f"b{bk}", bufs=1)
+                words = prod[i][:].rearrange("p u r e -> p (u r e)").bitcast(F32)
+                for u in range(2):
+                    nc.tensor.transpose(bank[:, u, :], words[:, u * P : (u + 1) * P], ident[:])
+                bank_of[i] = bank
+                return
+            bank = psum.tile([P, 2, 2, P], F32, name="t_bank", tag=f"b{bk}", bufs=1)
+            for k, src in enumerate((f_t, y_t)):
+                words = src[m, g // 2][:].bitcast(F32)
+                a = 256 * (g % 2)
+                for u in range(2):
+                    nc.tensor.transpose(bank[:, k, u, :], words[:, a + u : a + 256 : 2], ident[:])
+            bank_of[i] = bank
+
+        def gather(i):
+            t = work.tile([P, P, 2, 2], BF16, name="grouped", bufs=6, align_bytes=64)
+            nc.scalar.copy(
+                out=t[:].rearrange("p r u e -> p (r u e)").bitcast(F32).rearrange("p (r u) -> p r u", u=2),
+                in_=bank_of[i][:].rearrange("p u r -> p r u"),
+            )
+            grouped[i] = t
+
+        def by_word(i, k):
+            return (
+                bank_of[i][:]
+                .rearrange("p k u r -> p (k u r)")[:, 256 * k : 256 * (k + 1)]
+                .bitcast(BF16)
+                .rearrange("p (u r e) -> p r u e", u=2, e=2)
+            )
+
+        def by_parity(src, i):
+            m, g = passes[i]
+            a = 512 * (g % 2)
+            return src[m, g // 2][:, a : a + 512].rearrange("p (r u e) -> p u r e", u=2, e=2)
+
+        def invert(i):
+            shape = [P, 2, P, 2] if i in UNFUSED else [P, P, 2, 2]
+            r = work.tile(shape, F32, name="recip", bufs=6)
+            src = by_parity(f_t, i) if i in UNFUSED else by_word(i, 0)
+            nc.scalar.activation(out=r[:], in_=src, func=ACT.Abs_reciprocal_sqrt)
+            nc.scalar.activation(out=r[:], in_=r[:], func=ACT.Square)
+            recip[i] = r
+
+        def divide(i):
+            if i in UNFUSED:
+                t = work.tile([P, 2, P, 2], BF16, name="prod", bufs=6, align_bytes=64)
+                nc.vector.tensor_tensor(out=t[:], in0=by_parity(y_t, i), in1=recip[i][:], op=MULT)
+                prod[i] = t
+                return
+            t = work.tile([P, P, 2, 2], BF16, name="grouped", bufs=6, align_bytes=64)
+            nc.vector.tensor_tensor(out=t[:], in0=by_word(i, 1), in1=recip[i][:], op=MULT)
+            grouped[i] = t
+
+        def quantize_ratio(i):
+            codes = keep.tile([P, P], U32, name=f"rc{i}", align_bytes=64)
+            scales = keep.tile([P, P], U8, name=f"rs{i}", align_bytes=64)
+            nc.vector.quantize_mx(
+                out=codes[:].bitcast(FP8X4), scales=scales[:], in_=grouped[i][:].rearrange("p r u e -> p (r u e)")
+            )
+            r_codes[passes[i]], r_scales[passes[i]] = codes, scales
+
+        def spread(n, g, engine):
+            t = work.tile([P, N, 4], BF16, name="ad_grouped", align_bytes=64)
+            if FAST:
+                dst = t[:].rearrange("p (c i) t -> p c t i", i=4)
+                src = ad_raw[n, g][:].rearrange("p t (c i) -> p c t i", i=4)
+            else:
+                dst, src = t[:], ad_raw[n, g][:].rearrange("p j w -> p w j")
+            if engine == "S":
+                nc.scalar.copy(out=dst, in_=src)
+            else:
+                nc.vector.tensor_copy(out=dst, in_=src)
+            ad_grouped[n, g] = t
+
+        def quantize_ad(n, g):
+            codes = keep.tile([P, N], U32, name=f"ac{n}_{g}", align_bytes=64)
+            scales = keep.tile([P, N], U8, name=f"as{n}_{g}", align_bytes=64)
+            nc.vector.quantize_mx(
+                out=codes[:].bitcast(FP8X4), scales=scales[:], in_=ad_grouped[n, g][:].rearrange("p w j -> p (w j)")
+            )
+            ad_codes[n, g], ad_scales[n, g] = codes, scales
+
+        def scale_x(m, n, eng):
+            t = work.tile([P, N], F32, name="xs", bufs=16)
+            cols = slice(n * N, (n + 1) * N)
+            eng.tensor_tensor(out=t[:], in0=x_t[m][:, cols], in1=recip_sens[:, cols], op=MULT)
+            xs[m, n] = t
+
+        units = {}
+
+        def multiply(m, n, g, bk):
+            k = units.get((m, n), 0)
+            units[m, n] = k + 1
+            if k == 0:
+                acc[m, n] = psum.tile([P, N], F32, name="acc", tag=f"b{bk}", bufs=1)
+            if g < 4:
+                rhs = ao_t[g][:, 2 * n * N : 2 * (n + 1) * N].bitcast(FP4X4)
+                rhs_scale = ao_sc[:, g, n * N : (n + 1) * N]
+            else:
+                rhs = ad_codes[n, g - 4][:].bitcast(FP8X4)
+                rhs_scale = ad_scales[n, g - 4][:]
+            nc.tensor.matmul_mx(
+                out=acc[m, n][:],
+                lhsT=r_codes[m, g][:].bitcast(FP8X4),
+                lhsT_scale=r_scales[m, g][:],
+                rhs=rhs,
+                rhs_scale=rhs_scale,
+                start=(k == 0),
+                stop=(k == 5),
+            )
+
+        def finish(m, n):
+            nc.vector.tensor_tensor(out=xs[m, n][:], in0=acc[m, n][:], in1=xs[m, n][:], op=MULT)
+            nc.sync.dma_start(out=out[m * P : (m + 1) * P, n * N : (n + 1) * N], in_=xs[m, n][:])
+
+        with tc.manual_schedule():
+            for tok in SEQ.split():
+                k, v = tok[0], tok[1:]
+                v, bk = v.split(".") if "." in v else (v, "")
+                if k == "N": invert_sens()
+                if k == "R": spread_sens(int(v))
+                if k == "T": flip(int(v), bk)
+                if k == "C": gather(int(v))
+                if k == "I": invert(int(v))
+                if k == "D": divide(int(v))
+                if k == "Q": quantize_ratio(int(v))
+                if k == "S": spread(int(v[0]), int(v[1]), "S")
+                if k == "V": spread(int(v[0]), int(v[1]), "V")
+                if k == "A": quantize_ad(int(v[0]), int(v[1]))
+                if k == "X": scale_x(int(v[0]), int(v[1]), nc.vector)
+                if k == "G": scale_x(int(v[0]), int(v[1]), nc.gpsimd)
+                if k == "M": multiply(int(v[0]), int(v[1]), int(v[2]), bk)
+                if k == "F": finish(int(v[0]), int(v[1]))

@@ -17,19 +17,16 @@ P = 128
 FRAMES, KD, KO, VOXELS = 512, 1024, 2048, 2048
 FLOPS = 2 * FRAMES * (KD + KO) * VOXELS
 K_PASS = 512
-K_CHUNK = 1024
+CHUNK = 1024
 M_TILES = FRAMES // P
 N = 512
-N_TILES = VOXELS // N
-CHUNKS = (KO + KD) // K_CHUNK
-OBLIQUE_CHUNKS = KO // K_CHUNK
 
-LOADS = "f00 y00 d00 f01 y01 y10 d01 x1 y11 f02 x0 y02 f12 f10 y12 d10 f11 d21 a1 s d11 a2 y21 y20 a3 f20 a0 f21 y32 f32 y22 f22 f31 x3 y30 x2 f30 y31 d31 d20 d30"
-SEQ = "N R0 T0.0 R1 T1.1 I0 V00 I1 T2.2 D0 T3.3 A00 I2 Q0 D1 V01 I3 R2 Q1 A01 R3 D2 D3 Q2 Q3 X00 T4.4 X01 T5.5 I4 X02 T6.6 X03 T7.7 I5 D4 X10 I6 Q4 D5 M004.0 T8.1 V10 I7 T9.2 Q5 I8 A10 M005.0 T10.3 D6 I9 D7 T11.4 Q6 M001.0 Q7 D8 M011.5 I10 M014.5 D9 M021.6 M031.7 Q8 M101.1 Q9 I11 D10 M111.2 M002.0 V11 M012.5 M022.6 S21 M032.7 M102.1 M112.2 Q10 M121.3 A11 M104.1 M003.0 D11 M013.5 M015.5 X11 M023.6 I12 M033.7 Q11 M103.1 A21 M105.1 M000.0 X12 I13 M010.5 M020.6 F00 M025.6 M030.7 F01 I14 M100.1 M110.2 D12 M113.2 M114.2 F10 I15 T12.4 M115.2 D13 M120.3 F11 M122.3 C12 T13.0 I16 Q12 M123.3 D14 M125.3 D15 M130.5 C13 T14.1 I17 D16 M131.5 T15.4 Q13 T16.2 X13 M132.5 C14 M133.5 D17 C15 M200.0 C16 M201.0 Q14 I18 Q15 T17.1 Q16 X20 M202.0 M203.0 X21 M204.0 C17 M210.4 I19 D18 M211.4 M212.4 Q17 X22 T18.2 M205.0 I20 D19 M213.4 M214.4 F20 T19.1 C18 M215.4 D20 C19 M220.0 I21 F21 M221.0 T20.2 Q18 M222.0 Q19 V20 C20 M223.0 I22 M225.0 M230.1 M231.1 M232.1 Q20 I23 M233.1 A20 M300.4 M301.4 D21 M024.6 S31 M124.3 D22 T21.2 M224.0 F02 M302.4 F12 T22.6 F22 M310.3 M311.3 D23 C21 M312.3 C22 M320.0 A31 S30 T23.2 M321.0 Q21 Q22 X23 M035.7 M135.5 X30 M235.1 M303.4 X31 M304.4 M313.3 X32 M314.3 C23 M322.0 M323.0 Q23 A30 M305.4 M315.3 F30 M324.0 M034.7 F31 M134.5 M234.1 F03 M325.0 M330.6 F13 M331.6 M332.6 F23 M333.6 M334.6 F32 M335.6 X33 F33"
-ACC_BANKS = 7
-T_BANKS = 4
-UNFUSED = (12, 13, 14, 15, 16, 17, 18, 19, 20, 21, 22, 23)
-FAST = True
+LOADS = "F0 Y0 D0 D1 f0 y1 F1 s y0 Y1 f1 x01 a23 a01 F23 Y23 f23 y23 x23"
+SEQ = "N f0.0 f1.1 I0 R0.2 y0.3 Z0 J0 y1.4 R1.5 I1 D0 R2.6 R3.7 J1 Z1 Q0 Z2 Z3 D1 V00 S10 Q1 S11 V01 f2.0 A0 I2 f3.2 A1 f4.1 J2 V20 I3 V21 y2.3 J3 D2 I4 y3.5 y4.6 A2 J4 Q2 I5 D3 M002.7 M012.4 J5 D4 M022.0 S31 Q3 Q4 D5 M001.7 M011.4 X00 y5.2 S30 M021.0 X01 M031.3 M000.7 X10 M010.4 M020.0 C5 F00 M030.3 I6 F01 M100.1 F02 M101.1 J6 Q5 M110.5 A3 M102.1 I7 M111.5 D6 M032.3 J7 M112.5 F10 I8 y6.6 F03 M120.2 F11 J8 M121.2 X11 M122.2 C6 M130.7 D7 I9 M131.7 M132.7 F12 J9 y7.4 Q6 F13 M200.0 D8 C7 M210.1 I10 M220.3 Q7 y8.5 D9 J10 M201.0 X20 M211.1 C8 y9.6 I11 M221.3 X21 M230.2 J11 Q8 M231.2 D10 M202.0 C9 M212.1 F20 y10.7 F21 M222.3 C10 Q9 D11 M232.2 M300.4 F22 M310.5 F23 y11.6 M320.0 Q10 C11 X30 M301.4 M311.5 Q11 M321.0 X31 M302.4 M312.5 F30 M322.0 F31 M330.1 F32 M331.1 M332.1 F33"
+UNFUSED = (5, 6, 7, 8, 9, 10, 11)
+FAST = False
+R_BUFS = 4
+SENS_SCALAR = False
 
 
 def tile_pet_mlem_update_s1_kernel(tc, x, yd, fd, yo, fo, ad, ao_words, ao_scales, sens, out):
@@ -39,214 +36,275 @@ def tile_pet_mlem_update_s1_kernel(tc, x, yd, fd, yo, fo, ad, ao_words, ao_scale
         work = ctx.enter_context(tc.tile_pool(name="work", bufs=3))
         psum = ctx.enter_context(tc.psum_pool(name="psum", bufs=1))
 
-        ident = keep.tile([P, P], F32, name="ident")
-        make_identity(nc, ident[:])
-        ident_bf = keep.tile([P, P], BF16, name="ident_bf")
-        make_identity(nc, ident_bf[:])
         sens_rows = keep.tile([P, P], BF16, name="sens_rows")
         nc.vector.memset(sens_rows[:], 0.0)
-        ao_sc = keep.tile([P, 4, VOXELS], U8, name="ao_sc", align_bytes=64)
-        nc.gpsimd.memset(ao_sc[:].rearrange("p g n -> p (g n)").bitcast(I32), 0)
         warm = keep.tile([P, 1], F32, name="warm")
         nc.vector.memset(warm[:], 1.0)
         nc.scalar.activation(out=warm[:], in_=warm[:], func=ACT.Abs_reciprocal_sqrt)
+        ident_bf = keep.tile([P, P], BF16, name="ident_bf")
+        make_identity(nc, ident_bf[:])
+        ident = keep.tile([P, P], F32, name="ident")
+        make_identity(nc, ident[:])
+        plane = keep.tile([P, 4, VOXELS], U8, name="plane", align_bytes=64)
+        nc.gpsimd.memset(plane[:].rearrange("p g n -> p (g n)").bitcast(I32), 0)
 
-        y_t, f_t, ad_raw, ao_t, x_t = {}, {}, {}, {}, {}
+        ratio_in, ad_raw, ao_t, x_t = {}, {}, {}, {}
         nc.sync.dma_start(out=sens_rows[0:16, :], in_=sens.rearrange("(c p) -> c p", c=16))
 
-        def load_part(dst, oblique, direct, name, m, c):
-            src, col = (oblique, c) if c < OBLIQUE_CHUNKS else (direct, c - OBLIQUE_CHUNKS)
-            t = keep.tile([P, K_CHUNK], BF16, name=f"{name}{m}_{c}", align_bytes=64)
-            nc.sync.dma_start(
-                out=t[:], in_=src[m * P : (m + 1) * P, col * K_CHUNK : (col + 1) * K_CHUNK]
-            )
-            dst[m, c] = t
+        def by_frame(t):
+            return t.rearrange("(p r) k -> p r k", r=M_TILES)
 
-        def load_ad(n, g):
-            a = keep.tile([P, 4, N], BF16, name=f"ad{n}_{g}", align_bytes=64)
-            nc.sync.dma_start(
-                out=a[:],
-                in_=ad[g * K_PASS : (g + 1) * K_PASS, n * N : (n + 1) * N].rearrange("(p j) w -> p j w", j=4),
-            )
-            ad_raw[n, g] = a
-
-        def load_ao(g):
-            w = keep.tile([P, 2 * VOXELS], U8, name=f"ao{g}", align_bytes=64)
-            nc.sync.dma_start(out=w[:].bitcast(I32), in_=ao_words[g].bitcast(I32))
-            ao_t[g] = w
-
-        def load_ao_scales():
-            for q in range(4):
-                nc.sync.dma_start(
-                    out=ao_sc[32 * q : 32 * q + 4, :, :].bitcast(I32),
-                    in_=ao_scales[:, 4 * q : 4 * q + 4, :].rearrange("g r n -> r g n").bitcast(I32),
-                )
-
-        def load_x(m):
-            t = keep.tile([P, VOXELS], BF16, name=f"x{m}", align_bytes=64)
-            nc.sync.dma_start(out=t[:], in_=x[m * P : (m + 1) * P, :])
-            x_t[m] = t
+        def load(tok):
+            k = tok[0]
+            if k in "FYfy":
+                half = {"a": 0, "b": 1}.get(tok[-1])
+                ms = [int(ch) for ch in tok[1:] if ch not in "ab"]
+                src = by_frame({"F": fo, "Y": yo, "f": fd, "y": yd}[k])
+                width = KO if k in "FY" else KD
+                name = k.replace("F", "fo").replace("Y", "yo")
+                if (k, ms[0]) not in ratio_in:
+                    t = keep.tile([P, len(ms), width], BF16, name=f"{name}{ms[0]}", align_bytes=64)
+                    for r, m in enumerate(ms):
+                        ratio_in[k, m] = (t, r)
+                t = ratio_in[k, ms[0]][0]
+                cols = slice(0, width) if half is None else slice(half * CHUNK, (half + 1) * CHUNK)
+                nc.sync.dma_start(out=t[:, :, cols], in_=src[:, ms[0] : ms[-1] + 1, cols])
+            if k == "D":
+                g = int(tok[1])
+                if len(tok) == 2:
+                    n0, wide = 0, VOXELS
+                else:
+                    n0, wide = 2 * int(tok[2]), 2 * N
+                t = keep.tile([P, 4, wide], BF16, name="ad" + tok[1:], align_bytes=64)
+                src = ad[g * K_PASS : (g + 1) * K_PASS, n0 * N : n0 * N + wide]
+                nc.sync.dma_start(out=t[:], in_=src.rearrange("(p j) w -> p j w", j=4))
+                for i in range(wide // N):
+                    ad_raw[n0 + i, g] = t[:, :, i * N : (i + 1) * N]
+            if k == "a":
+                gs = [int(ch) for ch in tok[1:]]
+                t = keep.tile([P, len(gs), 2 * VOXELS], U8, name="ao" + tok[1:], align_bytes=64)
+                src = ao_words[gs[0] : gs[-1] + 1].rearrange("g p b -> p g b")
+                nc.sync.dma_start(out=t[:].bitcast(I32), in_=src.bitcast(I32))
+                for i, g in enumerate(gs):
+                    ao_t[g] = t[:, i, :]
+            if k == "s":
+                for q in range(4):
+                    nc.sync.dma_start(
+                        out=plane[32 * q : 32 * q + 4, :, :].bitcast(I32),
+                        in_=ao_scales[:, 4 * q : 4 * q + 4, :].rearrange("g r n -> r g n").bitcast(I32),
+                    )
+            if k == "x":
+                ms = [int(ch) for ch in tok[1:]]
+                t = keep.tile([P, len(ms), VOXELS], BF16, name="x" + tok[1:], align_bytes=64)
+                nc.sync.dma_start(out=t[:], in_=by_frame(x)[:, ms[0] : ms[-1] + 1, :])
+                for i, m in enumerate(ms):
+                    x_t[m] = t[:, i, :]
 
         for tok in LOADS.split():
-            k, v = tok[0], [int(ch) for ch in tok[1:]]
-            if k == "f": load_part(f_t, fo, fd, "f", *v)
-            if k == "y": load_part(y_t, yo, yd, "y", *v)
-            if k == "d": load_ad(*v)
-            if k == "a": load_ao(*v)
-            if k == "s": load_ao_scales()
-            if k == "x": load_x(*v)
+            load(tok)
 
-        passes = [(m, g) for m in range(M_TILES) for g in range(6)]
-        bank_of, recip, grouped, prod, r_codes, r_scales = {}, {}, {}, {}, {}, {}
+        chunks = [(m, c) for m in range(M_TILES) for c in range(3)]
+        f_bank, y_bank, recip, grouped, prod, r_codes, r_scales = {}, {}, {}, {}, {}, {}, {}
         ad_grouped, ad_codes, ad_scales, acc, xs = {}, {}, {}, {}, {}
         recip_sens = keep.tile([P, VOXELS], F32, name="recip_sens")
         recip_col = keep.tile([P, 16], F32, name="recip_col")
 
+        def bank_tile(bk, name, shape, dtype=F32):
+            return psum.tile(shape, dtype, name=name, tag=f"b{bk}", bufs=1)
+
+        def source(k, i):
+            m, c = chunks[i]
+            if c < 2:
+                t, r = ratio_in["F" if k == "f" else "Y", m]
+                return t[:, r, c * CHUNK : (c + 1) * CHUNK]
+            t, r = ratio_in[k, m]
+            return t[:, r, :]
+
         def invert_sens():
-            sens_t = psum.tile([P, P], BF16, name="sens_t", tag="b7", bufs=1)
+            sens_t = bank_tile(7, "sens_t", [P, P], BF16)
             nc.tensor.transpose(sens_t[:], sens_rows[:], ident_bf[:])
             nc.vector.reciprocal(out=recip_col[:], in_=sens_t[:, 0:16])
 
-        def spread_sens(n):
-            bank = psum.tile([P, 4, P], F32, name="s_bank", tag=f"b{7 - n}", bufs=1)
+        sens_bank = {}
+
+        def flip_sens(n, bk):
+            bank = bank_tile(bk, "s_bank", [P, 4, P])
             for i in range(4):
                 c = 4 * n + i
                 nc.tensor.transpose(bank[:, i, :], recip_col[:, c : c + 1].to_broadcast([P, P]), ident[:])
-            nc.scalar.copy(out=recip_sens[:, n * N : (n + 1) * N], in_=bank[:].rearrange("p i f -> p (i f)"))
+            sens_bank[n] = bank
 
-        def flip(i, bk):
-            m, g = passes[i]
+        def copy_sens(n):
+            dst, src = recip_sens[:, n * N : (n + 1) * N], sens_bank[n][:].rearrange("p i f -> p (i f)")
+            if SENS_SCALAR:
+                nc.scalar.copy(out=dst, in_=src)
+            else:
+                nc.vector.tensor_copy(out=dst, in_=src)
+
+        def flip(k, i, bk):
+            bank = bank_tile(bk, "t_bank", [P, 2, 2, P])
             if i in UNFUSED:
-                bank = psum.tile([P, 2, P], F32, name="p_bank", tag=f"b{bk}", bufs=1)
-                words = prod[i][:].rearrange("p u r e -> p (u r e)").bitcast(F32)
-                for u in range(2):
-                    nc.tensor.transpose(bank[:, u, :], words[:, u * P : (u + 1) * P], ident[:])
-                bank_of[i] = bank
-                return
-            bank = psum.tile([P, 2, 2, P], F32, name="t_bank", tag=f"b{bk}", bufs=1)
-            for k, src in enumerate((f_t, y_t)):
-                words = src[m, g // 2][:].bitcast(F32)
-                a = 256 * (g % 2)
-                for u in range(2):
-                    nc.tensor.transpose(bank[:, k, u, :], words[:, a + u : a + 256 : 2], ident[:])
-            bank_of[i] = bank
+                words = prod[i][:].rearrange("p u q e -> p (u q e)").bitcast(F32)
+            else:
+                words = source(k, i).bitcast(F32)
+            for u in range(2):
+                for h in range(2):
+                    if i in UNFUSED:
+                        a = 256 * u + 128 * h
+                        src = words[:, a : a + 128]
+                    else:
+                        src = words[:, 256 * h + u : 256 * (h + 1) : 2]
+                    nc.tensor.transpose(bank[:, u, h, :], src, ident[:])
+            (f_bank if k == "f" else y_bank)[i] = bank
+
+        def by_word(bank):
+            flat = bank[:].rearrange("p u h r -> p (u h r)").bitcast(BF16)
+            return flat.rearrange("p (u q e) -> p q u e", u=2, e=2)
+
+        def by_parity(src):
+            return src.rearrange("p (q u e) -> p u q e", u=2, e=2)
+
+        def new_grouped(i):
+            grouped[i] = work.tile([P, 256, 2, 2], BF16, name="grouped", align_bytes=64)
+            return grouped[i]
 
         def gather(i):
-            t = work.tile([P, P, 2, 2], BF16, name="grouped", bufs=6, align_bytes=64)
+            t = new_grouped(i)
             nc.scalar.copy(
-                out=t[:].rearrange("p r u e -> p (r u e)").bitcast(F32).rearrange("p (r u) -> p r u", u=2),
-                in_=bank_of[i][:].rearrange("p u r -> p r u"),
+                out=t[:].rearrange("p q u e -> p (q u e)").bitcast(F32).rearrange("p (q u) -> p q u", u=2),
+                in_=y_bank[i][:].rearrange("p u h r -> p (u h r)").rearrange("p (u q) -> p q u", u=2),
             )
-            grouped[i] = t
-
-        def by_word(i, k):
-            return (
-                bank_of[i][:]
-                .rearrange("p k u r -> p (k u r)")[:, 256 * k : 256 * (k + 1)]
-                .bitcast(BF16)
-                .rearrange("p (u r e) -> p r u e", u=2, e=2)
-            )
-
-        def by_parity(src, i):
-            m, g = passes[i]
-            a = 512 * (g % 2)
-            return src[m, g // 2][:, a : a + 512].rearrange("p (r u e) -> p u r e", u=2, e=2)
 
         def invert(i):
-            shape = [P, 2, P, 2] if i in UNFUSED else [P, P, 2, 2]
-            r = work.tile(shape, F32, name="recip", bufs=6)
-            src = by_parity(f_t, i) if i in UNFUSED else by_word(i, 0)
+            split = i in UNFUSED
+            r = work.tile([P, 2, 256, 2] if split else [P, 256, 2, 2], F32, name="recip", bufs=R_BUFS)
+            src = by_parity(source("f", i)) if split else by_word(f_bank[i])
             nc.scalar.activation(out=r[:], in_=src, func=ACT.Abs_reciprocal_sqrt)
-            nc.scalar.activation(out=r[:], in_=r[:], func=ACT.Square)
             recip[i] = r
+
+        def square(i):
+            r = recip[i]
+            nc.scalar.activation(out=r[:], in_=r[:], func=ACT.Square)
 
         def divide(i):
             if i in UNFUSED:
-                t = work.tile([P, 2, P, 2], BF16, name="prod", bufs=6, align_bytes=64)
-                nc.vector.tensor_tensor(out=t[:], in0=by_parity(y_t, i), in1=recip[i][:], op=MULT)
+                t = work.tile([P, 2, 256, 2], BF16, name="prod", bufs=2, align_bytes=64)
                 prod[i] = t
-                return
-            t = work.tile([P, P, 2, 2], BF16, name="grouped", bufs=6, align_bytes=64)
-            nc.vector.tensor_tensor(out=t[:], in0=by_word(i, 1), in1=recip[i][:], op=MULT)
-            grouped[i] = t
+                src = by_parity(source("y", i))
+            else:
+                t = new_grouped(i)
+                src = by_word(y_bank[i])
+            nc.vector.tensor_tensor(out=t[:], in0=src, in1=recip[i][:], op=MULT)
 
         def quantize_ratio(i):
-            codes = keep.tile([P, P], U32, name=f"rc{i}", align_bytes=64)
-            scales = keep.tile([P, P], U8, name=f"rs{i}", align_bytes=64)
+            codes = keep.tile([P, 256], U32, name=f"rc{i}", align_bytes=64)
+            scales = keep.tile([P, 256], U8, name=f"rs{i}", align_bytes=64)
             nc.vector.quantize_mx(
-                out=codes[:].bitcast(FP8X4), scales=scales[:], in_=grouped[i][:].rearrange("p r u e -> p (r u e)")
+                out=codes[:].bitcast(FP8X4), scales=scales[:], in_=grouped[i][:].rearrange("p q u e -> p (q u e)")
             )
-            r_codes[passes[i]], r_scales[passes[i]] = codes, scales
+            r_codes[chunks[i]], r_scales[chunks[i]] = codes, scales
 
         def spread(n, g, engine):
-            t = work.tile([P, N, 4], BF16, name="ad_grouped", align_bytes=64)
+            if n not in ad_grouped:
+                ad_grouped[n] = work.tile([P, 2, N, 4], BF16, name="ad_grouped", bufs=2, align_bytes=64)
+            t = ad_grouped[n][:, g, :, :]
+            raw = ad_raw[n, g]
             if FAST:
-                dst = t[:].rearrange("p (c i) t -> p c t i", i=4)
-                src = ad_raw[n, g][:].rearrange("p t (c i) -> p c t i", i=4)
+                dst = t.rearrange("p (c i) t -> p c t i", i=4)
+                src = raw.rearrange("p t (c i) -> p c t i", i=4)
             else:
-                dst, src = t[:], ad_raw[n, g][:].rearrange("p j w -> p w j")
+                dst, src = t, raw.rearrange("p j w -> p w j")
             if engine == "S":
                 nc.scalar.copy(out=dst, in_=src)
             else:
                 nc.vector.tensor_copy(out=dst, in_=src)
-            ad_grouped[n, g] = t
 
-        def quantize_ad(n, g):
-            codes = keep.tile([P, N], U32, name=f"ac{n}_{g}", align_bytes=64)
-            scales = keep.tile([P, N], U8, name=f"as{n}_{g}", align_bytes=64)
+        def quantize_ad(n):
+            codes = keep.tile([P, 2 * N], U32, name=f"ac{n}", align_bytes=64)
+            scales = keep.tile([P, 2 * N], U8, name=f"as{n}", align_bytes=64)
             nc.vector.quantize_mx(
-                out=codes[:].bitcast(FP8X4), scales=scales[:], in_=ad_grouped[n, g][:].rearrange("p w j -> p (w j)")
+                out=codes[:].bitcast(FP8X4), scales=scales[:], in_=ad_grouped[n][:].rearrange("p g w j -> p (g w j)")
             )
-            ad_codes[n, g], ad_scales[n, g] = codes, scales
+            ad_codes[n], ad_scales[n] = codes, scales
 
-        def scale_x(m, n, eng):
-            t = work.tile([P, N], F32, name="xs", bufs=16)
-            cols = slice(n * N, (n + 1) * N)
-            eng.tensor_tensor(out=t[:], in0=x_t[m][:, cols], in1=recip_sens[:, cols], op=MULT)
-            xs[m, n] = t
+        def scale_x(m, h, q=None):
+            if (m, h) not in xs:
+                xs[m, h] = work.tile([P, 2 * N], F32, name="xs", bufs=7)
+            t = xs[m, h]
+            a, w, eng = (0, 2 * N, nc.vector) if q is None else (256 * q, 256, nc.gpsimd)
+            cols = slice(2 * h * N + a, 2 * h * N + a + w)
+            eng.tensor_tensor(out=t[:, a : a + w], in0=x_t[m][:, cols], in1=recip_sens[:, cols], op=MULT)
 
         units = {}
 
-        def multiply(m, n, g, bk):
-            k = units.get((m, n), 0)
-            units[m, n] = k + 1
-            if k == 0:
-                acc[m, n] = psum.tile([P, N], F32, name="acc", tag=f"b{bk}", bufs=1)
-            if g < 4:
-                rhs = ao_t[g][:, 2 * n * N : 2 * (n + 1) * N].bitcast(FP4X4)
-                rhs_scale = ao_sc[:, g, n * N : (n + 1) * N]
-            else:
-                rhs = ad_codes[n, g - 4][:].bitcast(FP8X4)
-                rhs_scale = ad_scales[n, g - 4][:]
-            nc.tensor.matmul_mx(
-                out=acc[m, n][:],
-                lhsT=r_codes[m, g][:].bitcast(FP8X4),
-                lhsT_scale=r_scales[m, g][:],
-                rhs=rhs,
-                rhs_scale=rhs_scale,
-                start=(k == 0),
-                stop=(k == 5),
-            )
+        def multiply(m, n, c, bk):
+            done = units.get((m, n), 0)
+            units[m, n] = done + 1
+            if done == 0:
+                acc[m, n] = bank_tile(bk, "acc", [P, N])
+            for h in range(2):
+                if c < 2:
+                    g = 2 * c + h
+                    rhs = ao_t[g][:, 2 * n * N : 2 * (n + 1) * N].bitcast(FP4X4)
+                    rhs_scale = plane[:, g, n * N : (n + 1) * N]
+                else:
+                    rhs = ad_codes[n][:, h * N : (h + 1) * N].bitcast(FP8X4)
+                    rhs_scale = ad_scales[n][:, h * N : (h + 1) * N]
+                nc.tensor.matmul_mx(
+                    out=acc[m, n][:],
+                    lhsT=r_codes[m, c][:, h * P : (h + 1) * P].bitcast(FP8X4),
+                    lhsT_scale=r_scales[m, c][:, h * P : (h + 1) * P],
+                    rhs=rhs,
+                    rhs_scale=rhs_scale,
+                    start=(done == 0 and h == 0),
+                    stop=(done == 2 and h == 1),
+                )
+
+        half_done = {}
 
         def finish(m, n):
-            nc.vector.tensor_tensor(out=xs[m, n][:], in0=acc[m, n][:], in1=xs[m, n][:], op=MULT)
-            nc.sync.dma_start(out=out[m * P : (m + 1) * P, n * N : (n + 1) * N], in_=xs[m, n][:])
+            t = xs[m, n // 2]
+            part = t[:, (n % 2) * N : (n % 2 + 1) * N]
+            nc.vector.tensor_tensor(out=part, in0=acc[m, n][:], in1=part, op=MULT)
+            dst = by_frame(out)[:, m, :]
+            half_done[m, n // 2] = half_done.get((m, n // 2), 0) + 1
+            if m == M_TILES - 1 and n >= 2:
+                nc.sync.dma_start(out=dst[:, n * N : (n + 1) * N], in_=part)
+            elif half_done[m, n // 2] == 2:
+                h = n // 2
+                nc.sync.dma_start(out=dst[:, 2 * h * N : 2 * (h + 1) * N], in_=t[:])
 
         with tc.manual_schedule():
             for tok in SEQ.split():
                 k, v = tok[0], tok[1:]
                 v, bk = v.split(".") if "." in v else (v, "")
-                if k == "N": invert_sens()
-                if k == "R": spread_sens(int(v))
-                if k == "T": flip(int(v), bk)
-                if k == "C": gather(int(v))
-                if k == "I": invert(int(v))
-                if k == "D": divide(int(v))
-                if k == "Q": quantize_ratio(int(v))
-                if k == "S": spread(int(v[0]), int(v[1]), "S")
-                if k == "V": spread(int(v[0]), int(v[1]), "V")
-                if k == "A": quantize_ad(int(v[0]), int(v[1]))
-                if k == "X": scale_x(int(v[0]), int(v[1]), nc.vector)
-                if k == "G": scale_x(int(v[0]), int(v[1]), nc.gpsimd)
-                if k == "M": multiply(int(v[0]), int(v[1]), int(v[2]), bk)
-                if k == "F": finish(int(v[0]), int(v[1]))
+                if k == "N":
+                    invert_sens()
+                if k == "R":
+                    flip_sens(int(v), bk)
+                if k == "Z":
+                    copy_sens(int(v))
+                if k in "fy":
+                    flip(k, int(v), bk)
+                if k == "C":
+                    gather(int(v))
+                if k == "I":
+                    invert(int(v))
+                if k == "J":
+                    square(int(v))
+                if k == "D":
+                    divide(int(v))
+                if k == "Q":
+                    quantize_ratio(int(v))
+                if k in "SV":
+                    spread(int(v[0]), int(v[1]), k)
+                if k == "A":
+                    quantize_ad(int(v))
+                if k == "X":
+                    scale_x(int(v[0]), int(v[1]))
+                if k == "G":
+                    scale_x(int(v[0]), int(v[1]), int(v[2]))
+                if k == "M":
+                    multiply(int(v[0]), int(v[1]), int(v[2]), bk)
+                if k == "F":
+                    finish(int(v[0]), int(v[1]))

from contextlib import ExitStack

import concourse.mybir as mybir
from concourse.masks import make_identity

F32 = mybir.dt.float32
BF16 = mybir.dt.bfloat16
U32 = mybir.dt.uint32
I32 = mybir.dt.int32
U8 = mybir.dt.uint8
FP8X4 = mybir.dt.float8_e4m3fn_x4
FP4X4 = mybir.dt.float4_e2m1fn_x4
MULT = mybir.AluOpType.mult
ACT = mybir.ActivationFunctionType

P = 128
FRAMES, KD, KO, VOXELS = 512, 1024, 2048, 2048
FLOPS = 2 * FRAMES * (KD + KO) * VOXELS
K_PASS = 512
CHUNK = 1024
M_TILES = FRAMES // P
N = 512

LOADS = "F0 Y0 D0 D1 f0 y1 F1 s y0 Y1 f1 x01 a23 a01 F23 Y23 f23 y23 x23"
SEQ = "N f0.0 f1.1 I0 R0.2 y0.3 Z0 J0 y1.4 R1.5 I1 D0 R2.6 R3.7 J1 Z1 Q0 Z2 Z3 D1 V00 S10 Q1 S11 V01 f2.0 A0 I2 f3.2 A1 f4.1 J2 V20 I3 V21 y2.3 J3 D2 I4 y3.5 y4.6 A2 J4 Q2 I5 D3 M002.7 M012.4 J5 D4 M022.0 S31 Q3 Q4 D5 M001.7 M011.4 X00 y5.2 S30 M021.0 X01 M031.3 M000.7 X10 M010.4 M020.0 C5 F00 M030.3 I6 F01 M100.1 F02 M101.1 J6 Q5 M110.5 A3 M102.1 I7 M111.5 D6 M032.3 J7 M112.5 F10 I8 y6.6 F03 M120.2 F11 J8 M121.2 X11 M122.2 C6 M130.7 D7 I9 M131.7 M132.7 F12 J9 y7.4 Q6 F13 M200.0 D8 C7 M210.1 I10 M220.3 Q7 y8.5 D9 J10 M201.0 X20 M211.1 C8 y9.6 I11 M221.3 X21 M230.2 J11 Q8 M231.2 D10 M202.0 C9 M212.1 F20 y10.7 F21 M222.3 C10 Q9 D11 M232.2 M300.4 F22 M310.5 F23 y11.6 M320.0 Q10 C11 X30 M301.4 M311.5 Q11 M321.0 X31 M302.4 M312.5 F30 M322.0 F31 M330.1 F32 M331.1 M332.1 F33"
UNFUSED = (5, 6, 7, 8, 9, 10, 11)
FAST = False
R_BUFS = 4
SENS_SCALAR = False


def tile_pet_mlem_update_s1_kernel(tc, x, yd, fd, yo, fo, ad, ao_words, ao_scales, sens, out):
    nc = tc.nc
    with ExitStack() as ctx:
        keep = ctx.enter_context(tc.tile_pool(name="keep", bufs=1))
        work = ctx.enter_context(tc.tile_pool(name="work", bufs=3))
        psum = ctx.enter_context(tc.psum_pool(name="psum", bufs=1))

        sens_rows = keep.tile([P, P], BF16, name="sens_rows")
        nc.vector.memset(sens_rows[:], 0.0)
        warm = keep.tile([P, 1], F32, name="warm")
        nc.vector.memset(warm[:], 1.0)
        nc.scalar.activation(out=warm[:], in_=warm[:], func=ACT.Abs_reciprocal_sqrt)
        ident_bf = keep.tile([P, P], BF16, name="ident_bf")
        make_identity(nc, ident_bf[:])
        ident = keep.tile([P, P], F32, name="ident")
        make_identity(nc, ident[:])
        plane = keep.tile([P, 4, VOXELS], U8, name="plane", align_bytes=64)
        nc.gpsimd.memset(plane[:].rearrange("p g n -> p (g n)").bitcast(I32), 0)

        ratio_in, ad_raw, ao_t, x_t = {}, {}, {}, {}
        nc.sync.dma_start(out=sens_rows[0:16, :], in_=sens.rearrange("(c p) -> c p", c=16))

        def by_frame(t):
            return t.rearrange("(p r) k -> p r k", r=M_TILES)

        def load(tok):
            k = tok[0]
            if k in "FYfy":
                half = {"a": 0, "b": 1}.get(tok[-1])
                ms = [int(ch) for ch in tok[1:] if ch not in "ab"]
                src = by_frame({"F": fo, "Y": yo, "f": fd, "y": yd}[k])
                width = KO if k in "FY" else KD
                name = k.replace("F", "fo").replace("Y", "yo")
                if (k, ms[0]) not in ratio_in:
                    t = keep.tile([P, len(ms), width], BF16, name=f"{name}{ms[0]}", align_bytes=64)
                    for r, m in enumerate(ms):
                        ratio_in[k, m] = (t, r)
                t = ratio_in[k, ms[0]][0]
                cols = slice(0, width) if half is None else slice(half * CHUNK, (half + 1) * CHUNK)
                nc.sync.dma_start(out=t[:, :, cols], in_=src[:, ms[0] : ms[-1] + 1, cols])
            if k == "D":
                g = int(tok[1])
                if len(tok) == 2:
                    n0, wide = 0, VOXELS
                else:
                    n0, wide = 2 * int(tok[2]), 2 * N
                t = keep.tile([P, 4, wide], BF16, name="ad" + tok[1:], align_bytes=64)
                src = ad[g * K_PASS : (g + 1) * K_PASS, n0 * N : n0 * N + wide]
                nc.sync.dma_start(out=t[:], in_=src.rearrange("(p j) w -> p j w", j=4))
                for i in range(wide // N):
                    ad_raw[n0 + i, g] = t[:, :, i * N : (i + 1) * N]
            if k == "a":
                gs = [int(ch) for ch in tok[1:]]
                t = keep.tile([P, len(gs), 2 * VOXELS], U8, name="ao" + tok[1:], align_bytes=64)
                src = ao_words[gs[0] : gs[-1] + 1].rearrange("g p b -> p g b")
                nc.sync.dma_start(out=t[:].bitcast(I32), in_=src.bitcast(I32))
                for i, g in enumerate(gs):
                    ao_t[g] = t[:, i, :]
            if k == "s":
                for q in range(4):
                    nc.sync.dma_start(
                        out=plane[32 * q : 32 * q + 4, :, :].bitcast(I32),
                        in_=ao_scales[:, 4 * q : 4 * q + 4, :].rearrange("g r n -> r g n").bitcast(I32),
                    )
            if k == "x":
                ms = [int(ch) for ch in tok[1:]]
                t = keep.tile([P, len(ms), VOXELS], BF16, name="x" + tok[1:], align_bytes=64)
                nc.sync.dma_start(out=t[:], in_=by_frame(x)[:, ms[0] : ms[-1] + 1, :])
                for i, m in enumerate(ms):
                    x_t[m] = t[:, i, :]

        for tok in LOADS.split():
            load(tok)

        chunks = [(m, c) for m in range(M_TILES) for c in range(3)]
        f_bank, y_bank, recip, grouped, prod, r_codes, r_scales = {}, {}, {}, {}, {}, {}, {}
        ad_grouped, ad_codes, ad_scales, acc, xs = {}, {}, {}, {}, {}
        recip_sens = keep.tile([P, VOXELS], F32, name="recip_sens")
        recip_col = keep.tile([P, 16], F32, name="recip_col")

        def bank_tile(bk, name, shape, dtype=F32):
            return psum.tile(shape, dtype, name=name, tag=f"b{bk}", bufs=1)

        def source(k, i):
            m, c = chunks[i]
            if c < 2:
                t, r = ratio_in["F" if k == "f" else "Y", m]
                return t[:, r, c * CHUNK : (c + 1) * CHUNK]
            t, r = ratio_in[k, m]
            return t[:, r, :]

        def invert_sens():
            sens_t = bank_tile(7, "sens_t", [P, P], BF16)
            nc.tensor.transpose(sens_t[:], sens_rows[:], ident_bf[:])
            nc.vector.reciprocal(out=recip_col[:], in_=sens_t[:, 0:16])

        sens_bank = {}

        def flip_sens(n, bk):
            bank = bank_tile(bk, "s_bank", [P, 4, P])
            for i in range(4):
                c = 4 * n + i
                nc.tensor.transpose(bank[:, i, :], recip_col[:, c : c + 1].to_broadcast([P, P]), ident[:])
            sens_bank[n] = bank

        def copy_sens(n):
            dst, src = recip_sens[:, n * N : (n + 1) * N], sens_bank[n][:].rearrange("p i f -> p (i f)")
            if SENS_SCALAR:
                nc.scalar.copy(out=dst, in_=src)
            else:
                nc.vector.tensor_copy(out=dst, in_=src)

        def flip(k, i, bk):
            bank = bank_tile(bk, "t_bank", [P, 2, 2, P])
            if i in UNFUSED:
                words = prod[i][:].rearrange("p u q e -> p (u q e)").bitcast(F32)
            else:
                words = source(k, i).bitcast(F32)
            for u in range(2):
                for h in range(2):
                    if i in UNFUSED:
                        a = 256 * u + 128 * h
                        src = words[:, a : a + 128]
                    else:
                        src = words[:, 256 * h + u : 256 * (h + 1) : 2]
                    nc.tensor.transpose(bank[:, u, h, :], src, ident[:])
            (f_bank if k == "f" else y_bank)[i] = bank

        def by_word(bank):
            flat = bank[:].rearrange("p u h r -> p (u h r)").bitcast(BF16)
            return flat.rearrange("p (u q e) -> p q u e", u=2, e=2)

        def by_parity(src):
            return src.rearrange("p (q u e) -> p u q e", u=2, e=2)

        def new_grouped(i):
            grouped[i] = work.tile([P, 256, 2, 2], BF16, name="grouped", align_bytes=64)
            return grouped[i]

        def gather(i):
            t = new_grouped(i)
            nc.scalar.copy(
                out=t[:].rearrange("p q u e -> p (q u e)").bitcast(F32).rearrange("p (q u) -> p q u", u=2),
                in_=y_bank[i][:].rearrange("p u h r -> p (u h r)").rearrange("p (u q) -> p q u", u=2),
            )

        def invert(i):
            split = i in UNFUSED
            r = work.tile([P, 2, 256, 2] if split else [P, 256, 2, 2], F32, name="recip", bufs=R_BUFS)
            src = by_parity(source("f", i)) if split else by_word(f_bank[i])
            nc.scalar.activation(out=r[:], in_=src, func=ACT.Abs_reciprocal_sqrt)
            recip[i] = r

        def square(i):
            r = recip[i]
            nc.scalar.activation(out=r[:], in_=r[:], func=ACT.Square)

        def divide(i):
            if i in UNFUSED:
                t = work.tile([P, 2, 256, 2], BF16, name="prod", bufs=2, align_bytes=64)
                prod[i] = t
                src = by_parity(source("y", i))
            else:
                t = new_grouped(i)
                src = by_word(y_bank[i])
            nc.vector.tensor_tensor(out=t[:], in0=src, in1=recip[i][:], op=MULT)

        def quantize_ratio(i):
            codes = keep.tile([P, 256], U32, name=f"rc{i}", align_bytes=64)
            scales = keep.tile([P, 256], U8, name=f"rs{i}", align_bytes=64)
            nc.vector.quantize_mx(
                out=codes[:].bitcast(FP8X4), scales=scales[:], in_=grouped[i][:].rearrange("p q u e -> p (q u e)")
            )
            r_codes[chunks[i]], r_scales[chunks[i]] = codes, scales

        def spread(n, g, engine):
            if n not in ad_grouped:
                ad_grouped[n] = work.tile([P, 2, N, 4], BF16, name="ad_grouped", bufs=2, align_bytes=64)
            t = ad_grouped[n][:, g, :, :]
            raw = ad_raw[n, g]
            if FAST:
                dst = t.rearrange("p (c i) t -> p c t i", i=4)
                src = raw.rearrange("p t (c i) -> p c t i", i=4)
            else:
                dst, src = t, raw.rearrange("p j w -> p w j")
            if engine == "S":
                nc.scalar.copy(out=dst, in_=src)
            else:
                nc.vector.tensor_copy(out=dst, in_=src)

        def quantize_ad(n):
            codes = keep.tile([P, 2 * N], U32, name=f"ac{n}", align_bytes=64)
            scales = keep.tile([P, 2 * N], U8, name=f"as{n}", align_bytes=64)
            nc.vector.quantize_mx(
                out=codes[:].bitcast(FP8X4), scales=scales[:], in_=ad_grouped[n][:].rearrange("p g w j -> p (g w j)")
            )
            ad_codes[n], ad_scales[n] = codes, scales

        def scale_x(m, h, q=None):
            if (m, h) not in xs:
                xs[m, h] = work.tile([P, 2 * N], F32, name="xs", bufs=7)
            t = xs[m, h]
            a, w, eng = (0, 2 * N, nc.vector) if q is None else (256 * q, 256, nc.gpsimd)
            cols = slice(2 * h * N + a, 2 * h * N + a + w)
            eng.tensor_tensor(out=t[:, a : a + w], in0=x_t[m][:, cols], in1=recip_sens[:, cols], op=MULT)

        units = {}

        def multiply(m, n, c, bk):
            done = units.get((m, n), 0)
            units[m, n] = done + 1
            if done == 0:
                acc[m, n] = bank_tile(bk, "acc", [P, N])
            for h in range(2):
                if c < 2:
                    g = 2 * c + h
                    rhs = ao_t[g][:, 2 * n * N : 2 * (n + 1) * N].bitcast(FP4X4)
                    rhs_scale = plane[:, g, n * N : (n + 1) * N]
                else:
                    rhs = ad_codes[n][:, h * N : (h + 1) * N].bitcast(FP8X4)
                    rhs_scale = ad_scales[n][:, h * N : (h + 1) * N]
                nc.tensor.matmul_mx(
                    out=acc[m, n][:],
                    lhsT=r_codes[m, c][:, h * P : (h + 1) * P].bitcast(FP8X4),
                    lhsT_scale=r_scales[m, c][:, h * P : (h + 1) * P],
                    rhs=rhs,
                    rhs_scale=rhs_scale,
                    start=(done == 0 and h == 0),
                    stop=(done == 2 and h == 1),
                )

        half_done = {}

        def finish(m, n):
            t = xs[m, n // 2]
            part = t[:, (n % 2) * N : (n % 2 + 1) * N]
            nc.vector.tensor_tensor(out=part, in0=acc[m, n][:], in1=part, op=MULT)
            dst = by_frame(out)[:, m, :]
            half_done[m, n // 2] = half_done.get((m, n // 2), 0) + 1
            if m == M_TILES - 1 and n >= 2:
                nc.sync.dma_start(out=dst[:, n * N : (n + 1) * N], in_=part)
            elif half_done[m, n // 2] == 2:
                h = n // 2
                nc.sync.dma_start(out=dst[:, 2 * h * N : 2 * (h + 1) * N], in_=t[:])

        with tc.manual_schedule():
            for tok in SEQ.split():
                k, v = tok[0], tok[1:]
                v, bk = v.split(".") if "." in v else (v, "")
                if k == "N":
                    invert_sens()
                if k == "R":
                    flip_sens(int(v), bk)
                if k == "Z":
                    copy_sens(int(v))
                if k in "fy":
                    flip(k, int(v), bk)
                if k == "C":
                    gather(int(v))
                if k == "I":
                    invert(int(v))
                if k == "J":
                    square(int(v))
                if k == "D":
                    divide(int(v))
                if k == "Q":
                    quantize_ratio(int(v))
                if k in "SV":
                    spread(int(v[0]), int(v[1]), k)
                if k == "A":
                    quantize_ad(int(v))
                if k == "X":
                    scale_x(int(v[0]), int(v[1]))
                if k == "G":
                    scale_x(int(v[0]), int(v[1]), int(v[2]))
                if k == "M":
                    multiply(int(v[0]), int(v[1]), int(v[2]), bk)
                if k == "F":
                    finish(int(v[0]), int(v[1]))
